import numpy as np
import ml_dtypes


def mxq(x, axis, fmt="e4m3"):
    dtype, down = {"e4m3": (ml_dtypes.float8_e4m3fn, 7), "e5m2": (ml_dtypes.float8_e5m2, 14)}[fmt]
    v = np.moveaxis(np.asarray(x, np.float32).astype(ml_dtypes.bfloat16).astype(np.float64), axis, -1)
    blocks = v.reshape(v.shape[:-1] + (-1, 32))
    amax = np.abs(blocks).max(-1, keepdims=True)
    byte = np.maximum(np.where(amax > 0, np.frexp(amax)[1] - 1 + 127, 0) - down, 1)
    scale = np.exp2(byte - 127.0)
    codes = (blocks / scale).astype(np.float32).astype(dtype).astype(np.float64)
    return np.moveaxis((codes * scale).reshape(v.shape), -1, axis)


WIDE = False


def mx_kscale(k):
    if not WIDE:
        return np.ones(k)
    levels = np.array([10, -10, 5, -5, 0])
    if k % 512:
        return np.exp2(np.random.permutation(np.resize(levels, k // 32))).repeat(32)
    a = np.empty((k // 512, 16))
    for p in range(k // 512):
        a[p, :8] = np.random.permutation(np.resize(levels, 8))
        for g in range(8):
            far = levels[np.abs(levels - a[p, g]) >= 10]
            a[p, g + 8] = far[np.random.randint(len(far))]
    return np.exp2(a.ravel()).repeat(32)


def f64(x):
    return np.asarray(x).astype(np.float64)


def striped(idx):
    return np.tile(idx.reshape(-1, 16).T, (8, 1)).astype(np.uint16)


def unstriped(offs):
    return offs[:16].T.reshape(-1).astype(np.int64)


E2M1 = np.array([0.0, 0.5, 1.0, 1.5, 2.0, 3.0, 4.0, 6.0, -0.0, -0.5, -1.0, -1.5, -2.0, -3.0, -4.0, -6.0])


def pack_weight(w, fmt):
    k, n = w.shape
    w = f64(np.asarray(w, np.float32).astype(ml_dtypes.bfloat16)).reshape(k // 32, 32, n)
    amax = np.abs(w).max(1)
    if fmt == "e4m3":
        byte = np.frexp(amax)[1] - 1 + 127 - 7
    else:
        mant, ex = np.frexp(amax / 6.0)
        byte = np.where(mant > 0.5, ex, ex - 1) + 127
    byte = np.clip(np.where(amax > 0, byte, 1), 1, 254)
    scaled = (w * np.exp2(127.0 - byte)[:, None, :]).reshape(k, n).astype(np.float32)
    by_word = np.ascontiguousarray(scaled.reshape(k // 512, 128, 4, n).transpose(0, 1, 3, 2))
    if fmt == "e4m3":
        words = by_word.astype(ml_dtypes.float8_e4m3fn).view(np.uint8)
    else:
        c = by_word.astype(ml_dtypes.float4_e2m1fn).view(np.uint8) & 0xF
        words = (c[..., 0::2] | (c[..., 1::2] << 4)).reshape(k // 512, 128, 2 * n)
    return np.ascontiguousarray(words), np.ascontiguousarray(byte.astype(np.uint8).reshape(k // 512, 16, n))


def unpack_weight(words, scales, fmt):
    g, _, n = scales.shape
    words = np.ascontiguousarray(words).reshape(g, 128, n, -1)
    if fmt == "e4m3":
        vals = words.view(ml_dtypes.float8_e4m3fn).astype(np.float64)
    else:
        nib = np.empty((g, 128, n, 4), np.uint8)
        nib[..., 0::2] = words & 0xF
        nib[..., 1::2] = words >> 4
        vals = E2M1[nib]
    vals = vals * np.repeat(np.exp2(scales.astype(np.float64) - 127.0), 8, axis=1)[..., None]
    return vals.transpose(0, 1, 3, 2).reshape(g * 512, n)


def planes(y):
    n, m = y.shape
    v = y.astype(np.float32).astype(ml_dtypes.bfloat16).astype(np.float64).reshape(n // 32, 32, m)
    top = np.abs(v).max(1)
    byte = np.clip(np.where(top > 0, np.frexp(top)[1] - 1 + 127 - 7, 1), 1, 254)
    codes = (v * np.exp2(127.0 - byte)[:, None, :]).reshape(n, m).astype(np.float32).astype(ml_dtypes.float8_e4m3fn).view(np.uint8)
    words = codes.reshape(n // 512, 128, 4, m).transpose(0, 1, 3, 2)
    return np.ascontiguousarray(words), np.ascontiguousarray(byte.astype(np.uint8).reshape(n // 512, 16, m))


def silu(v):
    return v / (1.0 + np.exp(-np.maximum(v, -700.0)))


K, T, E, C, H, N = 1024, 512, 4, 128, 512, 512


def by_expert(wq, xq):
    return np.concatenate([wq[e].T @ xq[:, e * C:(e + 1) * C] for e in range(E)], axis=1)


def setup_inputs():
    n = np.random.standard_normal
    s = mx_kscale(K)
    u = mx_kscale(H)
    slot_token = np.random.permutation(T)[:E * C]
    x = pack_weight(n((K, T)) * s[:, None], "e4m3")
    w = pack_weight(n((K, N)) / np.sqrt(K) / s[:, None], "e2m1")
    return {
        "x_words": x[0],
        "x_scales": x[1],
        "w_words": w[0],
        "w_scales": w[1],
        "wa": (n((E, K, H)) / np.sqrt(K) / s[None, :, None] * u).astype(np.float32),
        "wb": (n((E, H, N)) / np.sqrt(H) / u[None, :, None]).astype(np.float32),
        "gate": np.tile(np.random.uniform(0.2, 1.0, E * C), (128, 1)).astype(np.float32),
        "offs": striped(slot_token),
    }


def reference(x_words, x_scales, w_words, w_scales, wa, wb, gate, offs):
    w = unpack_weight(w_words, w_scales, "e2m1")
    waq = mxq(f64(wa), 1, "e4m3")
    wbq = mxq(f64(wb), 1, "e4m3")
    idx = unstriped(offs)
    x = unpack_weight(x_words, x_scales, "e4m3")
    base = w.T @ x
    h = silu(by_expert(waq, x[:, idx]))
    y = by_expert(wbq, mxq(h, 0, "e4m3"))
    c = np.zeros((N, T))
    c[:, idx] = f64(gate[:1]) * y
    out_0 = base + c
    return (out_0,) + planes(out_0)

@@ -1,0 +1,283 @@
+from contextlib import ExitStack
+
+import concourse.mybir as mybir
+
+K, T, E, C, H, N = 1024, 512, 4, 128, 512, 512
+FLOPS = 2 * T * K * N + 2 * E * C * (K * H + H * N)
+
+F32 = mybir.dt.float32
+BF16 = mybir.dt.bfloat16
+I32 = mybir.dt.int32
+U32 = mybir.dt.uint32
+U16 = mybir.dt.uint16
+U8 = mybir.dt.uint8
+FP8X4 = mybir.dt.float8_e4m3fn_x4
+FP4X4 = mybir.dt.float4_e2m1fn_x4
+MULT = mybir.AluOpType.mult
+ADD = mybir.AluOpType.add
+COPY = mybir.ActivationFunctionType.Copy
+SILU = mybir.ActivationFunctionType.Silu
+
+P = 128
+PACK = 4
+PASS = P * PACK
+X_PASSES = K // PASS
+LIST_COLS = C // 16
+GATHER = 256
+
+
+def tile_moe_adp_silu_kernel(
+    tc, x_words, x_scales, w_words, w_scales, wa, wb, gate, offs, out_0, out_1, out_2
+):
+    nc = tc.nc
+    with ExitStack() as ctx:
+        held = ctx.enter_context(tc.tile_pool(name="held", bufs=1))
+        psum = ctx.enter_context(tc.psum_pool(name="psum", bufs=1))
+
+        def sb(shape, dtype, name, tag=""):
+            return held.tile(shape, dtype, name=name, tag=tag or name, align_bytes=64)
+
+        offsets = held.tile([P, E * LIST_COLS], U16, name="offsets")
+        xw = sb([P, X_PASSES * T], U32, "xw")
+        xs = sb([P, X_PASSES * T], U8, "xs")
+        ww_raw = sb([P, X_PASSES, 2 * N], U8, "ww_raw")
+        ws_raw = sb([P, X_PASSES, N], U8, "ws_raw")
+        ww = sb([P, X_PASSES, 2 * N], U8, "ww")
+        ws = sb([P, X_PASSES, N], U8, "ws")
+        gate_sb = sb([P, E * C], F32, "gate_sb")
+        xg = sb([P, X_PASSES * E * C], U32, "xg")
+        xgs = sb([P, X_PASSES * E * C], U8, "xgs")
+        routed = [sb([P, T], F32, "routed%d" % d) for d in range(PACK)]
+        result = sb([P, PACK, T], F32, "result")
+        base = [psum.tile([P, T], F32, name="base%d" % d) for d in range(PACK)]
+
+        nc.vector.memset(xs[:].bitcast(I32), 0)
+        nc.vector.memset(ws_raw[:].rearrange("p s n -> p (s n)").bitcast(I32), 0)
+
+        def load_matrix(rows, name):
+            raw = sb([P, PACK, rows.shape[1]], F32, name)
+            nc.sync.dma_start(out=raw[:], in_=rows.rearrange("(p j) c -> p j c", j=PACK))
+            return raw
+
+        def load_wa(e, s):
+            return load_matrix(wa[e, s * PASS : (s + 1) * PASS, :], "wa_raw%d_%d" % (e, s))
+
+        def quadrant(q, rows):
+            return slice(32 * q, 32 * q + rows)
+
+        nc.sync.dma_start(offsets[:], offs)
+        nc.sync.dma_start(
+            out=xw[:].bitcast(I32).rearrange("p (s t) -> p s t", s=X_PASSES),
+            in_=x_words.rearrange("s p t d -> p s (t d)").bitcast(I32),
+        )
+        nc.sync.dma_start(out=ww_raw[:].bitcast(I32), in_=w_words.rearrange("s p b -> p s b").bitcast(I32))
+        for q in range(4):
+            nc.sync.dma_start(
+                out=xs[quadrant(q, 4), :].bitcast(I32).rearrange("r (s t) -> r s t", s=X_PASSES),
+                in_=x_scales[:, 4 * q : 4 * q + 4, :].rearrange("s r t -> r s t").bitcast(I32),
+            )
+        wa_raw = {}
+        wb_raw = {}
+        wa_raw[0, 0] = load_wa(0, 0)
+        wa_raw[0, 1] = load_wa(0, 1)
+        for q in range(4):
+            nc.sync.dma_start(
+                out=ws_raw[quadrant(q, 4), :, :].bitcast(I32),
+                in_=w_scales[:, 4 * q : 4 * q + 4, :].rearrange("s r n -> r s n").bitcast(I32),
+            )
+        wb_raw[0] = [load_matrix(wb[0], "wb_raw0")]
+        nc.sync.dma_start(out=gate_sb[:], in_=gate)
+        wa_raw[1, 0] = load_wa(1, 0)
+        wa_raw[1, 1] = load_wa(1, 1)
+        wb_raw[1] = [load_matrix(wb[1], "wb_raw1")]
+        wa_raw[2, 0] = load_wa(2, 0)
+        wa_raw[2, 1] = load_wa(2, 1)
+        wb_raw[2] = [load_matrix(wb[2], "wb_raw2")]
+        wa_raw[3, 0] = load_wa(3, 0)
+        wa_raw[3, 1] = load_wa(3, 1)
+        wb_raw[3] = [load_matrix(wb[3][:, u * (N // 2) : (u + 1) * (N // 2)], "wb_raw3_%d" % u) for u in range(2)]
+
+        def gather(part):
+            lst = offsets[:, part * GATHER // 16 : (part + 1) * GATHER // 16]
+            for gathered, table in ((xg, xw), (xgs, xs)):
+                for s in range(X_PASSES):
+                    nc.vector.tensor_copy(
+                        gathered[:, s * T + part * GATHER : s * T + (part + 1) * GATHER],
+                        table[:, s * T : (s + 1) * T].indirect(lst),
+                    )
+
+        def deal(raws, rounded, pair, on_scalar):
+            m0 = 0
+            for raw in raws:
+                width = raw.shape[2] // PACK
+                src = raw[:].rearrange("p j (m t) -> p m j t", t=PACK)[:, :, :, 2 * pair : 2 * pair + 2]
+                dst = rounded[:, 2 * pair : 2 * pair + 2, m0 : m0 + width, :].rearrange("p t m j -> p m j t")
+                if on_scalar:
+                    nc.scalar.copy(dst, src)
+                else:
+                    nc.vector.tensor_copy(dst, src)
+                m0 = m0 + width
+
+        def round_matrix(raws, name, scalar_pairs):
+            rounded = sb([P, PACK, P, PACK], BF16, name)
+            for pair in range(2):
+                deal(raws, rounded, pair, pair in scalar_pairs)
+            return rounded
+
+        def quantize(rounded_flat, name, calls=1, tag=""):
+            words = rounded_flat.shape[1] // PACK
+            codes = sb([P, words], U32, name + "_codes", tag)
+            scales = sb([P, words], U8, name + "_scales")
+            step = words // calls
+            for c in range(calls):
+                nc.vector.quantize_mx(
+                    out=codes[:, c * step : (c + 1) * step].bitcast(FP8X4),
+                    scales=scales[:, c * step : (c + 1) * step],
+                    in_=rounded_flat[:, c * step * PACK : (c + 1) * step * PACK],
+                )
+            return codes, scales
+
+        def flat(rounded):
+            return rounded[:].rearrange("p t m j -> p (t m j)")
+
+        def first(acc, e, s, wa_q):
+            codes, scales = wa_q
+            for t in range(PACK):
+                cols = slice(t * P, (t + 1) * P)
+                slots = slice(s * T + e * C, s * T + (e + 1) * C)
+                nc.tensor.matmul_mx(
+                    out=acc[:, t, :],
+                    lhsT=codes[:, cols].bitcast(FP8X4),
+                    lhsT_scale=scales[:, cols],
+                    rhs=xg[:, slots].bitcast(FP8X4),
+                    rhs_scale=xgs[:, slots],
+                    start=(s == 0 and t == 0),
+                    stop=(s == X_PASSES - 1 and t == PACK - 1),
+                )
+
+        def second(out, d, wb_q, h_q):
+            cols = slice(d * P, (d + 1) * P)
+            nc.tensor.matmul_mx(
+                out=out,
+                lhsT=wb_q[0][:, cols].bitcast(FP8X4),
+                lhsT_scale=wb_q[1][:, cols],
+                rhs=h_q[0][:].bitcast(FP8X4),
+                rhs_scale=h_q[1][:],
+                start=True,
+                stop=True,
+            )
+
+        def frozen_words():
+            nc.scalar.copy(
+                ww[:].bitcast(U16).rearrange("p s (t m) -> p s t m", t=PACK),
+                ww_raw[:].bitcast(U16).rearrange("p s (m t) -> p s t m", t=PACK),
+            )
+
+        def frozen_scales():
+            nc.vector.tensor_copy(
+                ws[:].rearrange("p s (t m) -> p s t m", t=PACK),
+                ws_raw[:].rearrange("p s (m t) -> p s t m", t=PACK),
+            )
+
+        def frozen_products():
+            for d in range(PACK):
+                for s in range(X_PASSES):
+                    nc.tensor.matmul_mx(
+                        out=base[d][:],
+                        lhsT=ww[:, s, 2 * d * P : 2 * (d + 1) * P].bitcast(FP4X4),
+                        lhsT_scale=ws[:, s, d * P : (d + 1) * P],
+                        rhs=xw[:, s * T : (s + 1) * T].bitcast(FP8X4),
+                        rhs_scale=xs[:, s * T : (s + 1) * T],
+                        start=(s == 0),
+                        stop=(s == X_PASSES - 1),
+                    )
+
+        def lists(e):
+            return offsets[:, e * LIST_COLS : (e + 1) * LIST_COLS], gate_sb[:, e * C : (e + 1) * C]
+
+        def put_back(e, acc):
+            lst, gate_e = lists(e)
+            y = sb([P, PACK, C], F32, "y%d" % e, "wa_raw%d_0" % (e + 1))
+            nc.vector.tensor_tensor(y[:], acc[:], gate_e.unsqueeze(1).to_broadcast([P, PACK, C]), MULT)
+            for d in range(PACK):
+                nc.scalar.activation(routed[d][:].indirect(lst), y[:, d, :], COPY)
+
+        gather(0)
+        frozen_words()
+        gather(1)
+        y_acc = None
+        for e in range(E):
+            last = e == E - 1
+            rounded = round_matrix([wa_raw[e, 0]], "wa_bf%d_0" % e, (0, 1) if e == 0 else (1,))
+            if e > 0:
+                put_back(e - 1, y_acc)
+            h_acc = psum.tile([P, PACK, C], F32, name="h_acc%d" % e, tag="h_acc", bufs=2)
+            first(h_acc, e, 0, quantize(flat(rounded), "wa%d_0" % e))
+            rounded = round_matrix([wa_raw[e, 1]], "wa_bf%d_1" % e, (1,) if e == 0 else ())
+            first(h_acc, e, 1, quantize(flat(rounded), "wa%d_1" % e))
+            if e == 0:
+                frozen_scales()
+            rounded = round_matrix(wb_raw[e], "wb_bf%d" % e, (1,) if e == 0 else ())
+            h = sb([P, C, PACK], BF16, "h%d" % e)
+            nc.scalar.activation(h[:], h_acc[:].rearrange("p t c -> p c t"), SILU)
+            wb_q = quantize(flat(rounded), "wb%d" % e, calls=PACK if last else 1)
+            h_q = quantize(h[:].rearrange("p c t -> p (c t)"), "h%d" % e, tag="wb_raw3_1" if last else "wb_raw%d" % e)
+            if not last:
+                y_acc = psum.tile([P, PACK, C], F32, name="y_acc%d" % e, tag="y_acc", bufs=2)
+                for d in range(PACK):
+                    second(y_acc[:, d, :], d, wb_q, h_q)
+
+        lst, gate_e = lists(E - 1)
+        y = sb([P, PACK, C], F32, "y_last")
+        accs = [
+            psum.tile([P, C], F32, name="y_last%d" % d, tag=("y_acc", "h_acc")[d % 2], bufs=2) for d in range(PACK)
+        ]
+        for d in range(PACK):
+            second(accs[d][:], d, wb_q, h_q)
+        for d in range(PACK - 1):
+            nc.vector.tensor_tensor(y[:, d, :], accs[d][:], gate_e, MULT)
+        d = PACK - 1
+        nc.scalar.copy(y[:, d, :], accs[d][:])
+        for d in range(PACK - 1):
+            nc.scalar.activation(routed[d][:].indirect(lst), y[:, d, :], COPY)
+        d = PACK - 1
+        nc.vector.tensor_tensor(routed[d][:].indirect(lst), y[:, d, :], gate_e, MULT)
+
+        frozen_products()
+        out_rows = out_0.rearrange("(p d) t -> p d t", d=PACK)
+        half = T // 2
+        for d in (3, 0, 1):
+            nc.vector.tensor_tensor(result[:, d, :], base[d][:], routed[d][:], ADD)
+            nc.sync.dma_start(out=out_rows[:, d, :], in_=result[:, d, :])
+        d = 2
+        for u in range(2):
+            cols = slice(u * half, (u + 1) * half)
+            nc.vector.tensor_tensor(result[:, d, cols], base[d][:, cols], routed[d][:, cols], ADD)
+        nc.sync.dma_start(out=out_rows[:, d, :], in_=result[:, d, :])
+
+        codes = sb([P, T], U32, "out_codes")
+        scales = sb([P, T], U8, "out_scales")
+        rounded = [sb([P, half, PACK], BF16, "out_bf%d" % u) for u in range(2)]
+        for u in range(2):
+            cols = slice(u * half, (u + 1) * half)
+            dst = rounded[u][:].rearrange("p (c i) d -> p c d i", i=4)
+            src = result[:, :, cols].rearrange("p d (c i) -> p c d i", i=4)
+            if u == 0:
+                nc.scalar.copy(dst, src)
+            else:
+                nc.vector.tensor_copy(dst, src)
+        out_words = out_1[0].rearrange("p t d -> p (t d)").bitcast(I32)
+        for u in (1, 0):
+            cols = slice(u * half, (u + 1) * half)
+            nc.vector.quantize_mx(
+                out=codes[:, cols].bitcast(FP8X4),
+                scales=scales[:, cols],
+                in_=rounded[u][:].rearrange("p c d -> p (c d)"),
+            )
+            nc.sync.dma_start(out=out_words[:, cols], in_=codes[:, cols].bitcast(I32))
+        for q in range(4):
+            engine = (nc.scalar, nc.sync)[q % 2]
+            engine.dma_start(
+                out=out_2[0, 4 * q : 4 * q + 4, :].bitcast(I32),
+                in_=scales[quadrant(q, 4), :].bitcast(I32),
+            )

@@ -42,7 +42,6 @@ def tile_moe_adp_silu_kernel(
         xs = sb([P, X_PASSES * T], U8, "xs")
         ww_raw = sb([P, X_PASSES, 2 * N], U8, "ww_raw")
         ws_raw = sb([P, X_PASSES, N], U8, "ws_raw")
-        ww = sb([P, X_PASSES, 2 * N], U8, "ww")
         ws = sb([P, X_PASSES, N], U8, "ws")
         gate_sb = sb([P, E * C], F32, "gate_sb")
         xg = sb([P, X_PASSES * E * C], U32, "xg")
@@ -59,9 +58,6 @@ def tile_moe_adp_silu_kernel(
             nc.sync.dma_start(out=raw[:], in_=rows.rearrange("(p j) c -> p j c", j=PACK))
             return raw
 
-        def load_wa(e, s):
-            return load_matrix(wa[e, s * PASS : (s + 1) * PASS, :], "wa_raw%d_%d" % (e, s))
-
         def quadrant(q, rows):
             return slice(32 * q, 32 * q + rows)
 
@@ -70,32 +66,32 @@ def tile_moe_adp_silu_kernel(
             out=xw[:].bitcast(I32).rearrange("p (s t) -> p s t", s=X_PASSES),
             in_=x_words.rearrange("s p t d -> p s (t d)").bitcast(I32),
         )
-        nc.sync.dma_start(out=ww_raw[:].bitcast(I32), in_=w_words.rearrange("s p b -> p s b").bitcast(I32))
         for q in range(4):
             nc.sync.dma_start(
                 out=xs[quadrant(q, 4), :].bitcast(I32).rearrange("r (s t) -> r s t", s=X_PASSES),
                 in_=x_scales[:, 4 * q : 4 * q + 4, :].rearrange("s r t -> r s t").bitcast(I32),
             )
+        def load_halves(rows, name):
+            half_cols = rows.shape[1] // 2
+            return [load_matrix(rows[:, u * half_cols : (u + 1) * half_cols], "%s_%d" % (name, u)) for u in range(2)]
+
         wa_raw = {}
         wb_raw = {}
-        wa_raw[0, 0] = load_wa(0, 0)
-        wa_raw[0, 1] = load_wa(0, 1)
-        for q in range(4):
-            nc.sync.dma_start(
-                out=ws_raw[quadrant(q, 4), :, :].bitcast(I32),
-                in_=w_scales[:, 4 * q : 4 * q + 4, :].rearrange("s r n -> r s n").bitcast(I32),
-            )
-        wb_raw[0] = [load_matrix(wb[0], "wb_raw0")]
-        nc.sync.dma_start(out=gate_sb[:], in_=gate)
-        wa_raw[1, 0] = load_wa(1, 0)
-        wa_raw[1, 1] = load_wa(1, 1)
-        wb_raw[1] = [load_matrix(wb[1], "wb_raw1")]
-        wa_raw[2, 0] = load_wa(2, 0)
-        wa_raw[2, 1] = load_wa(2, 1)
-        wb_raw[2] = [load_matrix(wb[2], "wb_raw2")]
-        wa_raw[3, 0] = load_wa(3, 0)
-        wa_raw[3, 1] = load_wa(3, 1)
-        wb_raw[3] = [load_matrix(wb[3][:, u * (N // 2) : (u + 1) * (N // 2)], "wb_raw3_%d" % u) for u in range(2)]
+        for e in range(E):
+            wa_raw[e, 0] = load_halves(wa[e, 0:PASS, :], "wa_raw%d_0" % e)
+            wa_raw[e, 1] = [load_matrix(wa[e, PASS : 2 * PASS, :], "wa_raw%d_1" % e)]
+            if e == E - 1:
+                wb_raw[e] = load_halves(wb[e], "wb_raw%d" % e)
+            else:
+                wb_raw[e] = [load_matrix(wb[e], "wb_raw%d" % e)]
+            if e == 0:
+                for q in range(4):
+                    nc.sync.dma_start(
+                        out=ws_raw[quadrant(q, 4), :, :].bitcast(I32),
+                        in_=w_scales[:, 4 * q : 4 * q + 4, :].rearrange("s r n -> r s n").bitcast(I32),
+                    )
+                nc.sync.dma_start(out=gate_sb[:], in_=gate)
+                nc.sync.dma_start(out=ww_raw[:].bitcast(I32), in_=w_words.rearrange("s p b -> p s b").bitcast(I32))
 
         def gather(part):
             lst = offsets[:, part * GATHER // 16 : (part + 1) * GATHER // 16]
@@ -106,22 +102,18 @@ def tile_moe_adp_silu_kernel(
                         table[:, s * T : (s + 1) * T].indirect(lst),
                     )
 
-        def deal(raws, rounded, pair, on_scalar):
-            m0 = 0
-            for raw in raws:
-                width = raw.shape[2] // PACK
-                src = raw[:].rearrange("p j (m t) -> p m j t", t=PACK)[:, :, :, 2 * pair : 2 * pair + 2]
-                dst = rounded[:, 2 * pair : 2 * pair + 2, m0 : m0 + width, :].rearrange("p t m j -> p m j t")
-                if on_scalar:
-                    nc.scalar.copy(dst, src)
-                else:
-                    nc.vector.tensor_copy(dst, src)
-                m0 = m0 + width
-
-        def round_matrix(raws, name, scalar_pairs):
+        def round_matrix(raws, name, on_scalar):
             rounded = sb([P, PACK, P, PACK], BF16, name)
-            for pair in range(2):
-                deal(raws, rounded, pair, pair in scalar_pairs)
+            width = P // len(raws)
+            for u, raw in enumerate(raws):
+                shares = [(0, PACK)] if ((u, 0) in on_scalar) == ((u, 1) in on_scalar) else [(0, 2), (2, PACK)]
+                for lo, hi in shares:
+                    src = raw[:].rearrange("p j (m t) -> p m j t", t=PACK)[:, :, :, lo:hi]
+                    dst = rounded[:, lo:hi, u * width : (u + 1) * width, :].rearrange("p t m j -> p m j t")
+                    if (u, lo // 2) in on_scalar:
+                        nc.scalar.copy(dst, src)
+                    else:
+                        nc.vector.tensor_copy(dst, src)
             return rounded
 
         def quantize(rounded_flat, name, calls=1, tag=""):
@@ -167,11 +159,13 @@ def tile_moe_adp_silu_kernel(
                 stop=True,
             )
 
-        def frozen_words():
+        def frozen_words(pair, tag):
+            dealt = sb([P, X_PASSES, 2, 2 * P], U8, "ww%d" % pair, tag)
             nc.scalar.copy(
-                ww[:].bitcast(U16).rearrange("p s (t m) -> p s t m", t=PACK),
-                ww_raw[:].bitcast(U16).rearrange("p s (m t) -> p s t m", t=PACK),
+                dealt[:].bitcast(U16),
+                ww_raw[:].bitcast(U16).rearrange("p s (m t) -> p s t m", t=PACK)[:, :, 2 * pair : 2 * pair + 2, :],
             )
+            return dealt
 
         def frozen_scales():
             nc.vector.tensor_copy(
@@ -184,7 +178,7 @@ def tile_moe_adp_silu_kernel(
                 for s in range(X_PASSES):
                     nc.tensor.matmul_mx(
                         out=base[d][:],
-                        lhsT=ww[:, s, 2 * d * P : 2 * (d + 1) * P].bitcast(FP4X4),
+                        lhsT=ww[d // 2][:, s, d % 2, :].bitcast(FP4X4),
                         lhsT_scale=ws[:, s, d * P : (d + 1) * P],
                         rhs=xw[:, s * T : (s + 1) * T].bitcast(FP8X4),
                         rhs_scale=xs[:, s * T : (s + 1) * T],
@@ -197,32 +191,40 @@ def tile_moe_adp_silu_kernel(
 
         def put_back(e, acc):
             lst, gate_e = lists(e)
-            y = sb([P, PACK, C], F32, "y%d" % e, "wa_raw%d_0" % (e + 1))
+            y = sb([P, PACK, C], F32, "y%d" % e, "wa_raw%d_0_1" % (e + 1))
             nc.vector.tensor_tensor(y[:], acc[:], gate_e.unsqueeze(1).to_broadcast([P, PACK, C]), MULT)
             for d in range(PACK):
                 nc.scalar.activation(routed[d][:].indirect(lst), y[:, d, :], COPY)
 
         gather(0)
-        frozen_words()
         gather(1)
+        ww = []
         y_acc = None
+        first_half = [(0, 0), (0, 1)]
+        second_half = [(1, 0), (1, 1)]
         for e in range(E):
             last = e == E - 1
-            rounded = round_matrix([wa_raw[e, 0]], "wa_bf%d_0" % e, (0, 1) if e == 0 else (1,))
+            rounded = round_matrix(wa_raw[e, 0], "wa_bf%d_0" % e, first_half + second_half if e == 0 else first_half)
+            if e in (1, 2):
+                ww.append(frozen_words(e - 1, "wa_raw%d_0_0" % e))
             if e > 0:
                 put_back(e - 1, y_acc)
             h_acc = psum.tile([P, PACK, C], F32, name="h_acc%d" % e, tag="h_acc", bufs=2)
             first(h_acc, e, 0, quantize(flat(rounded), "wa%d_0" % e))
-            rounded = round_matrix([wa_raw[e, 1]], "wa_bf%d_1" % e, (1,) if e == 0 else ())
+            rounded = round_matrix(wa_raw[e, 1], "wa_bf%d_1" % e, [(0, 1)] if e == 0 else [])
             first(h_acc, e, 1, quantize(flat(rounded), "wa%d_1" % e))
+            rounded = round_matrix(wb_raw[e], "wb_bf%d" % e, [])
             if e == 0:
                 frozen_scales()
-            rounded = round_matrix(wb_raw[e], "wb_bf%d" % e, (1,) if e == 0 else ())
             h = sb([P, C, PACK], BF16, "h%d" % e)
             nc.scalar.activation(h[:], h_acc[:].rearrange("p t c -> p c t"), SILU)
-            wb_q = quantize(flat(rounded), "wb%d" % e, calls=PACK if last else 1)
-            h_q = quantize(h[:].rearrange("p c t -> p (c t)"), "h%d" % e, tag="wb_raw3_1" if last else "wb_raw%d" % e)
-            if not last:
+            h_flat = h[:].rearrange("p c t -> p (c t)")
+            if last:
+                h_q = quantize(h_flat, "h%d" % e, tag="wb_raw3_1")
+                wb_q = quantize(flat(rounded), "wb%d" % e, calls=PACK)
+            else:
+                wb_q = quantize(flat(rounded), "wb%d" % e)
+                h_q = quantize(h_flat, "h%d" % e, tag="wb_raw%d" % e)
                 y_acc = psum.tile([P, PACK, C], F32, name="y_acc%d" % e, tag="y_acc", bufs=2)
                 for d in range(PACK):
                     second(y_acc[:, d, :], d, wb_q, h_q)
@@ -234,22 +236,20 @@ def tile_moe_adp_silu_kernel(
         ]
         for d in range(PACK):
             second(accs[d][:], d, wb_q, h_q)
-        for d in range(PACK - 1):
+        nc.scalar.copy(y[:, 0, :], accs[0][:])
+        for d in range(1, PACK):
             nc.vector.tensor_tensor(y[:, d, :], accs[d][:], gate_e, MULT)
-        d = PACK - 1
-        nc.scalar.copy(y[:, d, :], accs[d][:])
-        for d in range(PACK - 1):
+        nc.vector.tensor_tensor(routed[0][:].indirect(lst), y[:, 0, :], gate_e, MULT)
+        for d in range(1, PACK):
             nc.scalar.activation(routed[d][:].indirect(lst), y[:, d, :], COPY)
-        d = PACK - 1
-        nc.vector.tensor_tensor(routed[d][:].indirect(lst), y[:, d, :], gate_e, MULT)
 
         frozen_products()
         out_rows = out_0.rearrange("(p d) t -> p d t", d=PACK)
         half = T // 2
-        for d in (3, 0, 1):
+        for d in range(PACK - 1):
             nc.vector.tensor_tensor(result[:, d, :], base[d][:], routed[d][:], ADD)
             nc.sync.dma_start(out=out_rows[:, d, :], in_=result[:, d, :])
-        d = 2
+        d = PACK - 1
         for u in range(2):
             cols = slice(u * half, (u + 1) * half)
             nc.vector.tensor_tensor(result[:, d, cols], base[d][:, cols], routed[d][:, cols], ADD)

@@ -1,6 +1,7 @@
 from contextlib import ExitStack
 
 import concourse.mybir as mybir
+from concourse.masks import make_identity
 
 K, T, E, C, H, N = 1024, 512, 4, 128, 512, 512
 FLOPS = 2 * T * K * N + 2 * E * C * (K * H + H * N)
@@ -24,6 +25,7 @@ PASS = P * PACK
 X_PASSES = K // PASS
 LIST_COLS = C // 16
 GATHER = 256
+SCALAR_SHARE = 64
 
 
 def tile_moe_adp_silu_kernel(
@@ -61,16 +63,19 @@ def tile_moe_adp_silu_kernel(
         def quadrant(q, rows):
             return slice(32 * q, 32 * q + rows)
 
-        nc.sync.dma_start(offsets[:], offs)
         nc.sync.dma_start(
             out=xw[:].bitcast(I32).rearrange("p (s t) -> p s t", s=X_PASSES),
             in_=x_words.rearrange("s p t d -> p s (t d)").bitcast(I32),
         )
+        nc.sync.dma_start(offsets[:], offs)
         for q in range(4):
             nc.sync.dma_start(
                 out=xs[quadrant(q, 4), :].bitcast(I32).rearrange("r (s t) -> r s t", s=X_PASSES),
                 in_=x_scales[:, 4 * q : 4 * q + 4, :].rearrange("s r t -> r s t").bitcast(I32),
             )
+        gate_rows = sb([P, C], F32, "gate_rows")
+        nc.sync.dma_start(out=gate_rows[:], in_=gate.rearrange("r (e c) -> (r e) c", e=E)[0:P, :])
+
         def load_halves(rows, name):
             half_cols = rows.shape[1] // 2
             return [load_matrix(rows[:, u * half_cols : (u + 1) * half_cols], "%s_%d" % (name, u)) for u in range(2)]
@@ -78,7 +83,7 @@ def tile_moe_adp_silu_kernel(
         wa_raw = {}
         wb_raw = {}
         for e in range(E):
-            wa_raw[e, 0] = load_halves(wa[e, 0:PASS, :], "wa_raw%d_0" % e)
+            wa_raw[e, 0] = [load_matrix(wa[e, 0:PASS, :], "wa_raw%d_0" % e)]
             wa_raw[e, 1] = [load_matrix(wa[e, PASS : 2 * PASS, :], "wa_raw%d_1" % e)]
             if e == E - 1:
                 wb_raw[e] = load_halves(wb[e], "wb_raw%d" % e)
@@ -90,7 +95,6 @@ def tile_moe_adp_silu_kernel(
                         out=ws_raw[quadrant(q, 4), :, :].bitcast(I32),
                         in_=w_scales[:, 4 * q : 4 * q + 4, :].rearrange("s r n -> r s n").bitcast(I32),
                     )
-                nc.sync.dma_start(out=gate_sb[:], in_=gate)
                 nc.sync.dma_start(out=ww_raw[:].bitcast(I32), in_=w_words.rearrange("s p b -> p s b").bitcast(I32))
 
         def gather(part):
@@ -106,15 +110,25 @@ def tile_moe_adp_silu_kernel(
             rounded = sb([P, PACK, P, PACK], BF16, name)
             width = P // len(raws)
             for u, raw in enumerate(raws):
-                shares = [(0, PACK)] if ((u, 0) in on_scalar) == ((u, 1) in on_scalar) else [(0, 2), (2, PACK)]
-                for lo, hi in shares:
-                    src = raw[:].rearrange("p j (m t) -> p m j t", t=PACK)[:, :, :, lo:hi]
-                    dst = rounded[:, lo:hi, u * width : (u + 1) * width, :].rearrange("p t m j -> p m j t")
-                    if (u, lo // 2) in on_scalar:
-                        nc.scalar.copy(dst, src)
-                    else:
-                        nc.vector.tensor_copy(dst, src)
+                src = raw[:].rearrange("p j (m t) -> p m j t", t=PACK)
+                dst = rounded[:, :, u * width : (u + 1) * width, :].rearrange("p t m j -> p m j t")
+                if on_scalar > 0:
+                    nc.scalar.copy(dst[:, 0:on_scalar], src[:, 0:on_scalar])
+                if on_scalar < width:
+                    nc.vector.tensor_copy(dst[:, on_scalar:width], src[:, on_scalar:width])
             return rounded
+
+        def spread_gate():
+            ident = sb([P, P], F32, "ident")
+            make_identity(nc, ident[:])
+            turned = psum.tile([P, P], F32, name="gate_turned", tag="y_acc", bufs=2)
+            nc.tensor.transpose(turned[:], gate_rows[:], ident[:])
+            columns = sb([P, E], F32, "gate_columns")
+            nc.scalar.copy(columns[:], turned[:, 0:E])
+            spread = psum.tile([P, E, C], F32, name="gate_spread", tag="y_acc", bufs=2)
+            for e in range(E):
+                nc.tensor.transpose(spread[:, e, :], columns[:, e : e + 1].to_broadcast([P, P]), ident[:])
+            nc.scalar.copy(gate_sb[:], spread[:].rearrange("p e c -> p (e c)"))
 
         def quantize(rounded_flat, name, calls=1, tag=""):
             words = rounded_flat.shape[1] // PACK
@@ -191,29 +205,26 @@ def tile_moe_adp_silu_kernel(
 
         def put_back(e, acc):
             lst, gate_e = lists(e)
-            y = sb([P, PACK, C], F32, "y%d" % e, "wa_raw%d_0_1" % (e + 1))
+            y = sb([P, PACK, C], F32, "y%d" % e, "wa_raw%d_0" % (e + 1))
             nc.vector.tensor_tensor(y[:], acc[:], gate_e.unsqueeze(1).to_broadcast([P, PACK, C]), MULT)
             for d in range(PACK):
                 nc.scalar.activation(routed[d][:].indirect(lst), y[:, d, :], COPY)
 
+        spread_gate()
         gather(0)
         gather(1)
         ww = []
         y_acc = None
-        first_half = [(0, 0), (0, 1)]
-        second_half = [(1, 0), (1, 1)]
         for e in range(E):
             last = e == E - 1
-            rounded = round_matrix(wa_raw[e, 0], "wa_bf%d_0" % e, first_half + second_half if e == 0 else first_half)
-            if e in (1, 2):
-                ww.append(frozen_words(e - 1, "wa_raw%d_0_0" % e))
+            rounded = round_matrix(wa_raw[e, 0], "wa_bf%d_0" % e, P if e == 0 else SCALAR_SHARE)
             if e > 0:
                 put_back(e - 1, y_acc)
             h_acc = psum.tile([P, PACK, C], F32, name="h_acc%d" % e, tag="h_acc", bufs=2)
             first(h_acc, e, 0, quantize(flat(rounded), "wa%d_0" % e))
-            rounded = round_matrix(wa_raw[e, 1], "wa_bf%d_1" % e, [(0, 1)] if e == 0 else [])
+            rounded = round_matrix(wa_raw[e, 1], "wa_bf%d_1" % e, SCALAR_SHARE if e == 0 else 0)
             first(h_acc, e, 1, quantize(flat(rounded), "wa%d_1" % e))
-            rounded = round_matrix(wb_raw[e], "wb_bf%d" % e, [])
+            rounded = round_matrix(wb_raw[e], "wb_bf%d" % e, 0)
             if e == 0:
                 frozen_scales()
             h = sb([P, C, PACK], BF16, "h%d" % e)
@@ -225,6 +236,8 @@ def tile_moe_adp_silu_kernel(
             else:
                 wb_q = quantize(flat(rounded), "wb%d" % e)
                 h_q = quantize(h_flat, "h%d" % e, tag="wb_raw%d" % e)
+                if e < 2:
+                    ww.append(frozen_words(e, "wb_bf%d" % e))
                 y_acc = psum.tile([P, PACK, C], F32, name="y_acc%d" % e, tag="y_acc", bufs=2)
                 for d in range(PACK):
                     second(y_acc[:, d, :], d, wb_q, h_q)

@@ -26,6 +26,7 @@ X_PASSES = K // PASS
 LIST_COLS = C // 16
 GATHER = 256
 SCALAR_SHARE = 64
+FIRST_SHARE = 128
 
 
 def tile_moe_adp_silu_kernel(
@@ -50,7 +51,7 @@ def tile_moe_adp_silu_kernel(
         xgs = sb([P, X_PASSES * E * C], U8, "xgs")
         routed = [sb([P, T], F32, "routed%d" % d) for d in range(PACK)]
         result = sb([P, PACK, T], F32, "result")
-        base = [psum.tile([P, T], F32, name="base%d" % d) for d in range(PACK)]
+        ww = sb([P, X_PASSES, 2 * N], U8, "ww")
 
         nc.vector.memset(xs[:].bitcast(I32), 0)
         nc.vector.memset(ws_raw[:].rearrange("p s n -> p (s n)").bitcast(I32), 0)
@@ -68,13 +69,13 @@ def tile_moe_adp_silu_kernel(
             in_=x_words.rearrange("s p t d -> p s (t d)").bitcast(I32),
         )
         nc.sync.dma_start(offsets[:], offs)
+        gate_rows = sb([P, C], F32, "gate_rows")
+        nc.sync.dma_start(out=gate_rows[:], in_=gate.rearrange("r (e c) -> (r e) c", e=E)[0:P, :])
         for q in range(4):
             nc.sync.dma_start(
                 out=xs[quadrant(q, 4), :].bitcast(I32).rearrange("r (s t) -> r s t", s=X_PASSES),
                 in_=x_scales[:, 4 * q : 4 * q + 4, :].rearrange("s r t -> r s t").bitcast(I32),
             )
-        gate_rows = sb([P, C], F32, "gate_rows")
-        nc.sync.dma_start(out=gate_rows[:], in_=gate.rearrange("r (e c) -> (r e) c", e=E)[0:P, :])
 
         def load_halves(rows, name):
             half_cols = rows.shape[1] // 2
@@ -83,49 +84,51 @@ def tile_moe_adp_silu_kernel(
         wa_raw = {}
         wb_raw = {}
         for e in range(E):
-            wa_raw[e, 0] = [load_matrix(wa[e, 0:PASS, :], "wa_raw%d_0" % e)]
-            wa_raw[e, 1] = [load_matrix(wa[e, PASS : 2 * PASS, :], "wa_raw%d_1" % e)]
-            if e == E - 1:
-                wb_raw[e] = load_halves(wb[e], "wb_raw%d" % e)
-            else:
-                wb_raw[e] = [load_matrix(wb[e], "wb_raw%d" % e)]
             if e == 0:
+                wa_raw[e, 0] = [load_matrix(wa[e, 0:PASS, :], "wa_raw%d_0" % e)]
+            else:
+                wa_raw[e, 0] = load_halves(wa[e, 0:PASS, :], "wa_raw%d_0" % e)
+            wa_raw[e, 1] = [load_matrix(wa[e, PASS : 2 * PASS, :], "wa_raw%d_1" % e)]
+            if e == 0:
+                nc.sync.dma_start(out=ww_raw[:].bitcast(I32), in_=w_words.rearrange("s p b -> p s b").bitcast(I32))
                 for q in range(4):
                     nc.sync.dma_start(
                         out=ws_raw[quadrant(q, 4), :, :].bitcast(I32),
                         in_=w_scales[:, 4 * q : 4 * q + 4, :].rearrange("s r n -> r s n").bitcast(I32),
                     )
-                nc.sync.dma_start(out=ww_raw[:].bitcast(I32), in_=w_words.rearrange("s p b -> p s b").bitcast(I32))
+            if e == E - 1:
+                wb_raw[e] = load_halves(wb[e], "wb_raw%d" % e)
+            else:
+                wb_raw[e] = [load_matrix(wb[e], "wb_raw%d" % e)]
 
-        def gather(part):
+        def gather(gathered, table, column, part):
             lst = offsets[:, part * GATHER // 16 : (part + 1) * GATHER // 16]
-            for gathered, table in ((xg, xw), (xgs, xs)):
-                for s in range(X_PASSES):
-                    nc.vector.tensor_copy(
-                        gathered[:, s * T + part * GATHER : s * T + (part + 1) * GATHER],
-                        table[:, s * T : (s + 1) * T].indirect(lst),
-                    )
+            nc.vector.tensor_copy(
+                gathered[:, column + part * GATHER : column + (part + 1) * GATHER],
+                table[:, column : column + T].indirect(lst),
+            )
 
         def round_matrix(raws, name, on_scalar):
             rounded = sb([P, PACK, P, PACK], BF16, name)
             width = P // len(raws)
-            for u, raw in enumerate(raws):
-                src = raw[:].rearrange("p j (m t) -> p m j t", t=PACK)
-                dst = rounded[:, :, u * width : (u + 1) * width, :].rearrange("p t m j -> p m j t")
-                if on_scalar > 0:
-                    nc.scalar.copy(dst[:, 0:on_scalar], src[:, 0:on_scalar])
-                if on_scalar < width:
-                    nc.vector.tensor_copy(dst[:, on_scalar:width], src[:, on_scalar:width])
+            for half, raw in enumerate(raws):
+                src = raw[:].rearrange("p (u e) (m t) -> p m u t e", e=2, t=PACK)
+                dst = rounded[:, :, half * width : (half + 1) * width, :].rearrange("p t m (u e) -> p m u t e", e=2)
+                split = min(max(on_scalar - half * width, 0), width)
+                if split > 0:
+                    nc.scalar.copy(dst[:, 0:split], src[:, 0:split])
+                if split < width:
+                    nc.vector.tensor_copy(dst[:, split:width], src[:, split:width])
             return rounded
 
         def spread_gate():
             ident = sb([P, P], F32, "ident")
             make_identity(nc, ident[:])
-            turned = psum.tile([P, P], F32, name="gate_turned", tag="y_acc", bufs=2)
+            turned = psum.tile([P, P], F32, name="gate_turned", tag="spare0")
             nc.tensor.transpose(turned[:], gate_rows[:], ident[:])
             columns = sb([P, E], F32, "gate_columns")
             nc.scalar.copy(columns[:], turned[:, 0:E])
-            spread = psum.tile([P, E, C], F32, name="gate_spread", tag="y_acc", bufs=2)
+            spread = psum.tile([P, E, C], F32, name="gate_spread", tag="spare1")
             for e in range(E):
                 nc.tensor.transpose(spread[:, e, :], columns[:, e : e + 1].to_broadcast([P, P]), ident[:])
             nc.scalar.copy(gate_sb[:], spread[:].rearrange("p e c -> p (e c)"))
@@ -173,13 +176,11 @@ def tile_moe_adp_silu_kernel(
                 stop=True,
             )
 
-        def frozen_words(pair, tag):
-            dealt = sb([P, X_PASSES, 2, 2 * P], U8, "ww%d" % pair, tag)
+        def frozen_words():
             nc.scalar.copy(
-                dealt[:].bitcast(U16),
-                ww_raw[:].bitcast(U16).rearrange("p s (m t) -> p s t m", t=PACK)[:, :, 2 * pair : 2 * pair + 2, :],
+                ww[:].bitcast(U16).rearrange("p s (t m) -> p s t m", t=PACK),
+                ww_raw[:].bitcast(U16).rearrange("p s (m t) -> p s t m", t=PACK),
             )
-            return dealt
 
         def frozen_scales():
             nc.vector.tensor_copy(
@@ -189,10 +190,11 @@ def tile_moe_adp_silu_kernel(
 
         def frozen_products():
             for d in range(PACK):
+                base.append(psum.tile([P, T], F32, name="base%d" % d, tag="base%d" % d))
                 for s in range(X_PASSES):
                     nc.tensor.matmul_mx(
                         out=base[d][:],
-                        lhsT=ww[d // 2][:, s, d % 2, :].bitcast(FP4X4),
+                        lhsT=ww[:, s, 2 * d * P : 2 * (d + 1) * P].bitcast(FP4X4),
                         lhsT_scale=ws[:, s, d * P : (d + 1) * P],
                         rhs=xw[:, s * T : (s + 1) * T].bitcast(FP8X4),
                         rhs_scale=xs[:, s * T : (s + 1) * T],
@@ -205,47 +207,59 @@ def tile_moe_adp_silu_kernel(
 
         def put_back(e, acc):
             lst, gate_e = lists(e)
-            y = sb([P, PACK, C], F32, "y%d" % e, "wa_raw%d_0" % (e + 1))
-            nc.vector.tensor_tensor(y[:], acc[:], gate_e.unsqueeze(1).to_broadcast([P, PACK, C]), MULT)
+            y = sb([P, PACK, C], F32, "y%d" % e, "wa_raw%d_0_1" % (e + 1))
+            for u in range(2):
+                nc.vector.tensor_tensor(
+                    y[:, 2 * u : 2 * u + 2, :], acc[u][:], gate_e.unsqueeze(1).to_broadcast([P, 2, C]), MULT
+                )
             for d in range(PACK):
                 nc.scalar.activation(routed[d][:].indirect(lst), y[:, d, :], COPY)
 
         spread_gate()
-        gather(0)
-        gather(1)
-        ww = []
+        for part in range(E * C // GATHER):
+            for gathered, table in ((xg, xw), (xgs, xs)):
+                for s in range(X_PASSES):
+                    gather(gathered, table, s * T, part)
         y_acc = None
         for e in range(E):
             last = e == E - 1
-            rounded = round_matrix(wa_raw[e, 0], "wa_bf%d_0" % e, P if e == 0 else SCALAR_SHARE)
+            rounded = round_matrix(wa_raw[e, 0], "wa_bf%d_0" % e, FIRST_SHARE if e == 0 else SCALAR_SHARE)
             if e > 0:
                 put_back(e - 1, y_acc)
-            h_acc = psum.tile([P, PACK, C], F32, name="h_acc%d" % e, tag="h_acc", bufs=2)
+            h_acc = psum.tile([P, PACK, C], F32, name="h_acc%d" % e, tag="h_acc%d" % (e % 2))
             first(h_acc, e, 0, quantize(flat(rounded), "wa%d_0" % e))
             rounded = round_matrix(wa_raw[e, 1], "wa_bf%d_1" % e, SCALAR_SHARE if e == 0 else 0)
             first(h_acc, e, 1, quantize(flat(rounded), "wa%d_1" % e))
-            rounded = round_matrix(wb_raw[e], "wb_bf%d" % e, 0)
             if e == 0:
+                frozen_words()
                 frozen_scales()
+            rounded = round_matrix(wb_raw[e], "wb_bf%d" % e, 0)
             h = sb([P, C, PACK], BF16, "h%d" % e)
             nc.scalar.activation(h[:], h_acc[:].rearrange("p t c -> p c t"), SILU)
             h_flat = h[:].rearrange("p c t -> p (c t)")
             if last:
-                h_q = quantize(h_flat, "h%d" % e, tag="wb_raw3_1")
-                wb_q = quantize(flat(rounded), "wb%d" % e, calls=PACK)
+                wb_q = (sb([P, N], U32, "wb_last_codes"), sb([P, N], U8, "wb_last_scales"))
+                for d in range(PACK):
+                    if d == 2:
+                        h_q = quantize(h_flat, "h%d" % e, tag="wb_raw3_1")
+                    nc.vector.quantize_mx(
+                        out=wb_q[0][:, d * P : (d + 1) * P].bitcast(FP8X4),
+                        scales=wb_q[1][:, d * P : (d + 1) * P],
+                        in_=rounded[:, d, :, :].rearrange("p m j -> p (m j)"),
+                    )
             else:
                 wb_q = quantize(flat(rounded), "wb%d" % e)
                 h_q = quantize(h_flat, "h%d" % e, tag="wb_raw%d" % e)
-                if e < 2:
-                    ww.append(frozen_words(e, "wb_bf%d" % e))
-                y_acc = psum.tile([P, PACK, C], F32, name="y_acc%d" % e, tag="y_acc", bufs=2)
+                tags = ["base%d" % (2 * e + u) if e < 2 else "spare%d" % u for u in range(2)]
+                y_acc = [psum.tile([P, 2, C], F32, name="y_acc%d_%d" % (e, u), tag=tags[u]) for u in range(2)]
                 for d in range(PACK):
-                    second(y_acc[:, d, :], d, wb_q, h_q)
+                    second(y_acc[d // 2][:, d % 2, :], d, wb_q, h_q)
 
         lst, gate_e = lists(E - 1)
         y = sb([P, PACK, C], F32, "y_last")
         accs = [
-            psum.tile([P, C], F32, name="y_last%d" % d, tag=("y_acc", "h_acc")[d % 2], bufs=2) for d in range(PACK)
+            psum.tile([P, C], F32, name="y_last%d" % d, tag=("spare0", "spare1", "h_acc0", "h_acc1")[d])
+            for d in range(PACK)
         ]
         for d in range(PACK):
             second(accs[d][:], d, wb_q, h_q)
@@ -256,6 +270,7 @@ def tile_moe_adp_silu_kernel(
         for d in range(1, PACK):
             nc.scalar.activation(routed[d][:].indirect(lst), y[:, d, :], COPY)
 
+        base = []
         frozen_products()
         out_rows = out_0.rearrange("(p d) t -> p d t", d=PACK)
         half = T // 2

from contextlib import ExitStack

import concourse.mybir as mybir
from concourse.masks import make_identity

K, T, E, C, H, N = 1024, 512, 4, 128, 512, 512
FLOPS = 2 * T * K * N + 2 * E * C * (K * H + H * N)

F32 = mybir.dt.float32
BF16 = mybir.dt.bfloat16
I32 = mybir.dt.int32
U32 = mybir.dt.uint32
U16 = mybir.dt.uint16
U8 = mybir.dt.uint8
FP8X4 = mybir.dt.float8_e4m3fn_x4
FP4X4 = mybir.dt.float4_e2m1fn_x4
MULT = mybir.AluOpType.mult
ADD = mybir.AluOpType.add
COPY = mybir.ActivationFunctionType.Copy
SILU = mybir.ActivationFunctionType.Silu

P = 128
PACK = 4
PASS = P * PACK
X_PASSES = K // PASS
LIST_COLS = C // 16
GATHER = 256
SCALAR_SHARE = 64
FIRST_SHARE = 128


def tile_moe_adp_silu_kernel(
    tc, x_words, x_scales, w_words, w_scales, wa, wb, gate, offs, out_0, out_1, out_2
):
    nc = tc.nc
    with ExitStack() as ctx:
        held = ctx.enter_context(tc.tile_pool(name="held", bufs=1))
        psum = ctx.enter_context(tc.psum_pool(name="psum", bufs=1))

        def sb(shape, dtype, name, tag=""):
            return held.tile(shape, dtype, name=name, tag=tag or name, align_bytes=64)

        offsets = held.tile([P, E * LIST_COLS], U16, name="offsets")
        xw = sb([P, X_PASSES * T], U32, "xw")
        xs = sb([P, X_PASSES * T], U8, "xs")
        ww_raw = sb([P, X_PASSES, 2 * N], U8, "ww_raw")
        ws_raw = sb([P, X_PASSES, N], U8, "ws_raw")
        ws = sb([P, X_PASSES, N], U8, "ws")
        gate_sb = sb([P, E * C], F32, "gate_sb")
        xg = sb([P, X_PASSES * E * C], U32, "xg")
        xgs = sb([P, X_PASSES * E * C], U8, "xgs")
        routed = [sb([P, T], F32, "routed%d" % d) for d in range(PACK)]
        result = sb([P, PACK, T], F32, "result")
        ww = sb([P, X_PASSES, 2 * N], U8, "ww")

        nc.vector.memset(xs[:].bitcast(I32), 0)
        nc.vector.memset(ws_raw[:].rearrange("p s n -> p (s n)").bitcast(I32), 0)

        def load_matrix(rows, name):
            raw = sb([P, PACK, rows.shape[1]], F32, name)
            nc.sync.dma_start(out=raw[:], in_=rows.rearrange("(p j) c -> p j c", j=PACK))
            return raw

        def quadrant(q, rows):
            return slice(32 * q, 32 * q + rows)

        nc.sync.dma_start(
            out=xw[:].bitcast(I32).rearrange("p (s t) -> p s t", s=X_PASSES),
            in_=x_words.rearrange("s p t d -> p s (t d)").bitcast(I32),
        )
        nc.sync.dma_start(offsets[:], offs)
        gate_rows = sb([P, C], F32, "gate_rows")
        nc.sync.dma_start(out=gate_rows[:], in_=gate.rearrange("r (e c) -> (r e) c", e=E)[0:P, :])
        for q in range(4):
            nc.sync.dma_start(
                out=xs[quadrant(q, 4), :].bitcast(I32).rearrange("r (s t) -> r s t", s=X_PASSES),
                in_=x_scales[:, 4 * q : 4 * q + 4, :].rearrange("s r t -> r s t").bitcast(I32),
            )

        def load_halves(rows, name):
            half_cols = rows.shape[1] // 2
            return [load_matrix(rows[:, u * half_cols : (u + 1) * half_cols], "%s_%d" % (name, u)) for u in range(2)]

        wa_raw = {}
        wb_raw = {}
        for e in range(E):
            if e == 0:
                wa_raw[e, 0] = [load_matrix(wa[e, 0:PASS, :], "wa_raw%d_0" % e)]
            else:
                wa_raw[e, 0] = load_halves(wa[e, 0:PASS, :], "wa_raw%d_0" % e)
            wa_raw[e, 1] = [load_matrix(wa[e, PASS : 2 * PASS, :], "wa_raw%d_1" % e)]
            if e == 0:
                nc.sync.dma_start(out=ww_raw[:].bitcast(I32), in_=w_words.rearrange("s p b -> p s b").bitcast(I32))
                for q in range(4):
                    nc.sync.dma_start(
                        out=ws_raw[quadrant(q, 4), :, :].bitcast(I32),
                        in_=w_scales[:, 4 * q : 4 * q + 4, :].rearrange("s r n -> r s n").bitcast(I32),
                    )
            if e == E - 1:
                wb_raw[e] = load_halves(wb[e], "wb_raw%d" % e)
            else:
                wb_raw[e] = [load_matrix(wb[e], "wb_raw%d" % e)]

        def gather(gathered, table, column, part):
            lst = offsets[:, part * GATHER // 16 : (part + 1) * GATHER // 16]
            nc.vector.tensor_copy(
                gathered[:, column + part * GATHER : column + (part + 1) * GATHER],
                table[:, column : column + T].indirect(lst),
            )

        def round_matrix(raws, name, on_scalar):
            rounded = sb([P, PACK, P, PACK], BF16, name)
            width = P // len(raws)
            for half, raw in enumerate(raws):
                src = raw[:].rearrange("p (u e) (m t) -> p m u t e", e=2, t=PACK)
                dst = rounded[:, :, half * width : (half + 1) * width, :].rearrange("p t m (u e) -> p m u t e", e=2)
                split = min(max(on_scalar - half * width, 0), width)
                if split > 0:
                    nc.scalar.copy(dst[:, 0:split], src[:, 0:split])
                if split < width:
                    nc.vector.tensor_copy(dst[:, split:width], src[:, split:width])
            return rounded

        def spread_gate():
            ident = sb([P, P], F32, "ident")
            make_identity(nc, ident[:])
            turned = psum.tile([P, P], F32, name="gate_turned", tag="spare0")
            nc.tensor.transpose(turned[:], gate_rows[:], ident[:])
            columns = sb([P, E], F32, "gate_columns")
            nc.scalar.copy(columns[:], turned[:, 0:E])
            spread = psum.tile([P, E, C], F32, name="gate_spread", tag="spare1")
            for e in range(E):
                nc.tensor.transpose(spread[:, e, :], columns[:, e : e + 1].to_broadcast([P, P]), ident[:])
            nc.scalar.copy(gate_sb[:], spread[:].rearrange("p e c -> p (e c)"))

        def quantize(rounded_flat, name, calls=1, tag=""):
            words = rounded_flat.shape[1] // PACK
            codes = sb([P, words], U32, name + "_codes", tag)
            scales = sb([P, words], U8, name + "_scales")
            step = words // calls
            for c in range(calls):
                nc.vector.quantize_mx(
                    out=codes[:, c * step : (c + 1) * step].bitcast(FP8X4),
                    scales=scales[:, c * step : (c + 1) * step],
                    in_=rounded_flat[:, c * step * PACK : (c + 1) * step * PACK],
                )
            return codes, scales

        def flat(rounded):
            return rounded[:].rearrange("p t m j -> p (t m j)")

        def first(acc, e, s, wa_q):
            codes, scales = wa_q
            for t in range(PACK):
                cols = slice(t * P, (t + 1) * P)
                slots = slice(s * T + e * C, s * T + (e + 1) * C)
                nc.tensor.matmul_mx(
                    out=acc[:, t, :],
                    lhsT=codes[:, cols].bitcast(FP8X4),
                    lhsT_scale=scales[:, cols],
                    rhs=xg[:, slots].bitcast(FP8X4),
                    rhs_scale=xgs[:, slots],
                    start=(s == 0 and t == 0),
                    stop=(s == X_PASSES - 1 and t == PACK - 1),
                )

        def second(out, d, wb_q, h_q):
            cols = slice(d * P, (d + 1) * P)
            nc.tensor.matmul_mx(
                out=out,
                lhsT=wb_q[0][:, cols].bitcast(FP8X4),
                lhsT_scale=wb_q[1][:, cols],
                rhs=h_q[0][:].bitcast(FP8X4),
                rhs_scale=h_q[1][:],
                start=True,
                stop=True,
            )

        def frozen_words():
            nc.scalar.copy(
                ww[:].bitcast(U16).rearrange("p s (t m) -> p s t m", t=PACK),
                ww_raw[:].bitcast(U16).rearrange("p s (m t) -> p s t m", t=PACK),
            )

        def frozen_scales():
            nc.vector.tensor_copy(
                ws[:].rearrange("p s (t m) -> p s t m", t=PACK),
                ws_raw[:].rearrange("p s (m t) -> p s t m", t=PACK),
            )

        def frozen_products():
            for d in range(PACK):
                base.append(psum.tile([P, T], F32, name="base%d" % d, tag="base%d" % d))
                for s in range(X_PASSES):
                    nc.tensor.matmul_mx(
                        out=base[d][:],
                        lhsT=ww[:, s, 2 * d * P : 2 * (d + 1) * P].bitcast(FP4X4),
                        lhsT_scale=ws[:, s, d * P : (d + 1) * P],
                        rhs=xw[:, s * T : (s + 1) * T].bitcast(FP8X4),
                        rhs_scale=xs[:, s * T : (s + 1) * T],
                        start=(s == 0),
                        stop=(s == X_PASSES - 1),
                    )

        def lists(e):
            return offsets[:, e * LIST_COLS : (e + 1) * LIST_COLS], gate_sb[:, e * C : (e + 1) * C]

        def put_back(e, acc):
            lst, gate_e = lists(e)
            y = sb([P, PACK, C], F32, "y%d" % e, "wa_raw%d_0_1" % (e + 1))
            for u in range(2):
                nc.vector.tensor_tensor(
                    y[:, 2 * u : 2 * u + 2, :], acc[u][:], gate_e.unsqueeze(1).to_broadcast([P, 2, C]), MULT
                )
            for d in range(PACK):
                nc.scalar.activation(routed[d][:].indirect(lst), y[:, d, :], COPY)

        spread_gate()
        for part in range(E * C // GATHER):
            for gathered, table in ((xg, xw), (xgs, xs)):
                for s in range(X_PASSES):
                    gather(gathered, table, s * T, part)
        y_acc = None
        for e in range(E):
            last = e == E - 1
            rounded = round_matrix(wa_raw[e, 0], "wa_bf%d_0" % e, FIRST_SHARE if e == 0 else SCALAR_SHARE)
            if e > 0:
                put_back(e - 1, y_acc)
            h_acc = psum.tile([P, PACK, C], F32, name="h_acc%d" % e, tag="h_acc%d" % (e % 2))
            first(h_acc, e, 0, quantize(flat(rounded), "wa%d_0" % e))
            rounded = round_matrix(wa_raw[e, 1], "wa_bf%d_1" % e, SCALAR_SHARE if e == 0 else 0)
            first(h_acc, e, 1, quantize(flat(rounded), "wa%d_1" % e))
            if e == 0:
                frozen_words()
                frozen_scales()
            rounded = round_matrix(wb_raw[e], "wb_bf%d" % e, 0)
            h = sb([P, C, PACK], BF16, "h%d" % e)
            nc.scalar.activation(h[:], h_acc[:].rearrange("p t c -> p c t"), SILU)
            h_flat = h[:].rearrange("p c t -> p (c t)")
            if last:
                wb_q = (sb([P, N], U32, "wb_last_codes"), sb([P, N], U8, "wb_last_scales"))
                for d in range(PACK):
                    if d == 2:
                        h_q = quantize(h_flat, "h%d" % e, tag="wb_raw3_1")
                    nc.vector.quantize_mx(
                        out=wb_q[0][:, d * P : (d + 1) * P].bitcast(FP8X4),
                        scales=wb_q[1][:, d * P : (d + 1) * P],
                        in_=rounded[:, d, :, :].rearrange("p m j -> p (m j)"),
                    )
            else:
                wb_q = quantize(flat(rounded), "wb%d" % e)
                h_q = quantize(h_flat, "h%d" % e, tag="wb_raw%d" % e)
                tags = ["base%d" % (2 * e + u) if e < 2 else "spare%d" % u for u in range(2)]
                y_acc = [psum.tile([P, 2, C], F32, name="y_acc%d_%d" % (e, u), tag=tags[u]) for u in range(2)]
                for d in range(PACK):
                    second(y_acc[d // 2][:, d % 2, :], d, wb_q, h_q)

        lst, gate_e = lists(E - 1)
        y = sb([P, PACK, C], F32, "y_last")
        accs = [
            psum.tile([P, C], F32, name="y_last%d" % d, tag=("spare0", "spare1", "h_acc0", "h_acc1")[d])
            for d in range(PACK)
        ]
        for d in range(PACK):
            second(accs[d][:], d, wb_q, h_q)
        nc.scalar.copy(y[:, 0, :], accs[0][:])
        for d in range(1, PACK):
            nc.vector.tensor_tensor(y[:, d, :], accs[d][:], gate_e, MULT)
        nc.vector.tensor_tensor(routed[0][:].indirect(lst), y[:, 0, :], gate_e, MULT)
        for d in range(1, PACK):
            nc.scalar.activation(routed[d][:].indirect(lst), y[:, d, :], COPY)

        base = []
        frozen_products()
        out_rows = out_0.rearrange("(p d) t -> p d t", d=PACK)
        half = T // 2
        for d in range(PACK - 1):
            nc.vector.tensor_tensor(result[:, d, :], base[d][:], routed[d][:], ADD)
            nc.sync.dma_start(out=out_rows[:, d, :], in_=result[:, d, :])
        d = PACK - 1
        for u in range(2):
            cols = slice(u * half, (u + 1) * half)
            nc.vector.tensor_tensor(result[:, d, cols], base[d][:, cols], routed[d][:, cols], ADD)
        nc.sync.dma_start(out=out_rows[:, d, :], in_=result[:, d, :])

        codes = sb([P, T], U32, "out_codes")
        scales = sb([P, T], U8, "out_scales")
        rounded = [sb([P, half, PACK], BF16, "out_bf%d" % u) for u in range(2)]
        for u in range(2):
            cols = slice(u * half, (u + 1) * half)
            dst = rounded[u][:].rearrange("p (c i) d -> p c d i", i=4)
            src = result[:, :, cols].rearrange("p d (c i) -> p c d i", i=4)
            if u == 0:
                nc.scalar.copy(dst, src)
            else:
                nc.vector.tensor_copy(dst, src)
        out_words = out_1[0].rearrange("p t d -> p (t d)").bitcast(I32)
        for u in (1, 0):
            cols = slice(u * half, (u + 1) * half)
            nc.vector.quantize_mx(
                out=codes[:, cols].bitcast(FP8X4),
                scales=scales[:, cols],
                in_=rounded[u][:].rearrange("p c d -> p (c d)"),
            )
            nc.sync.dma_start(out=out_words[:, cols], in_=codes[:, cols].bitcast(I32))
        for q in range(4):
            engine = (nc.scalar, nc.sync)[q % 2]
            engine.dma_start(
                out=out_2[0, 4 * q : 4 * q + 4, :].bitcast(I32),
                in_=scales[quadrant(q, 4), :].bitcast(I32),
            )
